import numpy as np
import ml_dtypes


def mxq(x, axis, fmt="e4m3"):
    dtype, down = {"e4m3": (ml_dtypes.float8_e4m3fn, 7), "e5m2": (ml_dtypes.float8_e5m2, 14)}[fmt]
    v = np.moveaxis(np.asarray(x, np.float32).astype(ml_dtypes.bfloat16).astype(np.float64), axis, -1)
    blocks = v.reshape(v.shape[:-1] + (-1, 32))
    amax = np.abs(blocks).max(-1, keepdims=True)
    byte = np.maximum(np.where(amax > 0, np.frexp(amax)[1] - 1 + 127, 0) - down, 1)
    scale = np.exp2(byte - 127.0)
    codes = (blocks / scale).astype(np.float32).astype(dtype).astype(np.float64)
    return np.moveaxis((codes * scale).reshape(v.shape), -1, axis)


WIDE = False


def mx_kscale(k):
    if not WIDE:
        return np.ones(k)
    levels = np.array([10, -10, 5, -5, 0])
    if k % 512:
        return np.exp2(np.random.permutation(np.resize(levels, k // 32))).repeat(32)
    a = np.empty((k // 512, 16))
    for p in range(k // 512):
        a[p, :8] = np.random.permutation(np.resize(levels, 8))
        for g in range(8):
            far = levels[np.abs(levels - a[p, g]) >= 10]
            a[p, g + 8] = far[np.random.randint(len(far))]
    return np.exp2(a.ravel()).repeat(32)


def f64(x):
    return np.asarray(x).astype(np.float64)


def striped(idx):
    return np.tile(idx.reshape(-1, 16).T, (8, 1)).astype(np.uint16)


def unstriped(offs):
    return offs[:16].T.reshape(-1).astype(np.int64)


def relu(v):
    return np.maximum(v, 0.0)


K, T, E, C, N = 1024, 1280, 15, 256, 128
TOP = 3


def by_expert(wq, xq):
    return np.concatenate([wq[e].T @ xq[:, e * C:(e + 1) * C] for e in range(E)], axis=1)


def setup_inputs():
    n = np.random.standard_normal
    s = mx_kscale(K)[:, None]
    deal = np.repeat(np.arange(E), C).reshape(TOP, T)[:, np.random.permutation(T)]
    deal = np.take_along_axis(deal, np.argsort(np.random.rand(TOP, T), axis=0), axis=0)
    for _ in range(8):
        s_, t_ = np.random.permutation(T).reshape(2, -1); r = np.random.randint(TOP, size=T // 2); x, y = deal[r, s_].copy(), deal[r, t_].copy()
        ok = ~((deal[:, s_] == y).any(0) | (deal[:, t_] == x).any(0)); deal[r[ok], s_[ok]] = y[ok]; deal[r[ok], t_[ok]] = x[ok]
    order = np.lexsort((np.random.rand(TOP * T), deal.reshape(-1)))
    slot_token = order % T; pos = np.empty(TOP * T, np.int64); pos[order] = np.arange(TOP * T); pos = pos.reshape(TOP, T)
    g = np.random.uniform(0.5, 1.5, (TOP, T)); g = g / g.sum(0)
    return {
        "xT": (n((K, T)) * s).astype(np.float32),
        "w": (n((E + 1, K, N)) / np.sqrt(K) / s[None]).astype(np.float32),
        "b": (0.3 * n((N, E + 1))).astype(np.float32),
        "gate": np.stack([np.tile(r, (N, 1)) for r in g]).astype(np.float32),
        "offs": striped(slot_token),
        "pos1": striped(pos[0]),
        "pos2": striped(pos[1]),
        "pos3": striped(pos[2]),
    }


def reference(xT, w, b, gate, offs, pos1, pos2, pos3):
    idx = unstriped(offs)
    wq = mxq(f64(w), 1, "e4m3")
    xs = mxq(f64(xT), 0, "e4m3")
    ys = relu((wq[E].T @ xs) + f64(b)[:, E:])
    xq = mxq(f64(xT)[:, idx], 0, "e4m3")
    y = by_expert(wq, xq)
    y = relu(y + np.repeat(f64(b)[:, :E], C, axis=1))
    return ys + sum(f64(gate[r]) * y[:, unstriped(p)] for r, p in enumerate((pos1, pos2, pos3)))

@@ -1,0 +1,202 @@
+from contextlib import ExitStack
+
+import concourse.mybir as mybir
+from concourse.masks import make_identity
+
+K, T, E, C, N = 1024, 1280, 15, 256, 128
+TOP = 3
+S = E * C
+FLOPS = 2 * K * N * (S + T)
+
+F32 = mybir.dt.float32
+BF16 = mybir.dt.bfloat16
+U32 = mybir.dt.uint32
+U16 = mybir.dt.uint16
+U8 = mybir.dt.uint8
+FP8X4 = mybir.dt.float8_e4m3fn_x4
+ACT = mybir.ActivationFunctionType
+ALU = mybir.AluOpType
+
+P = 128
+PASSES = 2
+EC = 3
+CH = EC * C
+NCH = E // EC
+AL = 64
+
+
+def widths(total):
+    out, at = [], 0
+    while at < total:
+        w = 4096
+        while w > total - at:
+            w //= 2
+        out.append((at, w))
+        at += w
+    return out
+
+
+def tile_moe_shr_lin_relu_kernel(tc, xT, w, b, gate, offs, pos1, pos2, pos3, out):
+    nc = tc.nc
+    with ExitStack() as ctx:
+        keep = ctx.enter_context(tc.tile_pool(name="keep", bufs=1))
+        ring = ctx.enter_context(tc.tile_pool(name="ring", bufs=1))
+        psum = ctx.enter_context(tc.psum_pool(name="psum", bufs=1))
+
+        def quantize(src, total, tag, width):
+            codes = ring.tile([P, width], U32, name=tag + "_codes", tag=tag + "_codes", bufs=2, align_bytes=AL)
+            scales = ring.tile([P, width], U8, name=tag + "_scales", tag=tag + "_scales", bufs=2, align_bytes=AL)
+            for at, wd in widths(total):
+                cols = slice(at // 4, (at + wd) // 4)
+                nc.vector.quantize_mx(out=codes[:, cols].bitcast(FP8X4), scales=scales[:, cols], in_=src[:, at:at + wd])
+            return codes, scales
+
+        offs_t = keep.tile([P, S // 16], U16, name="offs_t")
+        pos_t = [keep.tile([P, T // 16], U16, name="pos%d_t" % r) for r in range(TOP)]
+        bias = keep.tile([P, E + 1], F32, name="bias")
+        ident = keep.tile([P, P], F32, name="ident")
+        y = keep.tile([P, S], F32, name="y")
+        win = [keep.tile([P, 2, T, 2], BF16, name="win%d" % g, align_bytes=AL) for g in range(PASSES)]
+        x_rows = xT.rearrange("(g p u i) t -> g u p i t", g=PASSES, p=P, u=2)
+
+        def load_x(g, u, pieces):
+            raw = ring.tile([P, 2, T], F32, name="raw", tag="raw", bufs=3, align_bytes=AL)
+            for a, z in pieces:
+                nc.sync.dma_start(out=raw[:, :, a:z], in_=x_rows[g, u][:, :, a:z])
+            return raw
+
+        def words(g, u):
+            return win[g][:, u, :, :].rearrange("p t i -> p (t i)").bitcast(U32)
+
+        wb = {}
+
+        def load_w(e):
+            raw = ring.tile([P, PASSES, 4, N], F32, name="wraw", tag="wraw", bufs=4)
+            nc.sync.dma_start(out=raw[:], in_=w[e].rearrange("(g p j) n -> p g j n", g=PASSES, p=P))
+            c, i = divmod(e, EC)
+            if i == 0:
+                wb[c] = ring.tile([P, EC * PASSES * N * 4], BF16, name="wb", tag="wb", bufs=6, align_bytes=AL)
+            dst = wb[c][:, i * 1024:(i + 1) * 1024].rearrange("p (g n j) -> p g n j", g=PASSES, j=4)
+            nc.gpsimd.tensor_scalar(dst, raw[:].rearrange("p g j n -> p g n j"), 1.0, 0.0, ALU.mult, ALU.add)
+
+        gp = {}
+        xi = {}
+
+        def gather(g, u, c):
+            if u == 0:
+                gp[g, c] = ring.tile([P, 2, CH], U32, name="gp", tag="gp", bufs=4, align_bytes=AL)
+            nc.vector.tensor_copy(gp[g, c][:, u, :], words(g, u).indirect(offs_t[:, c * CH // 16:(c + 1) * CH // 16]))
+
+        def interleave(g, c):
+            if g == 0:
+                xi[c] = ring.tile([P, PASSES * CH * 4], BF16, name="xi", tag="xi", bufs=5, align_bytes=AL)
+            dst = xi[c][:, g * CH * 4:(g + 1) * CH * 4].bitcast(F32).rearrange("p (s u) -> p s u", u=2)
+            nc.scalar.copy(dst, gp[g, c][:].bitcast(F32).rearrange("p u s -> p s u"))
+
+        def cast_x(g, u, raw):
+            nc.scalar.activation(win[g][:, u, :, :], raw[:].rearrange("p i t -> p t i"), ACT.Copy)
+
+        first = [(0, 512), (512, 1024), (1024, T)]
+        raw00 = load_x(0, 0, first)
+        nc.sync.dma_start(offs_t[:], offs)
+        raw01 = load_x(0, 1, [(0, T)])
+        for a, z in first:
+            nc.vector.tensor_copy(win[0][:, 0, a:z, :], raw00[:, :, a:z].rearrange("p i t -> p t i"))
+        cast_x(0, 1, raw01)
+        for e in range(6):
+            load_w(e)
+        for c in range(3):
+            gather(0, 0, c)
+        raw10 = load_x(1, 0, [(0, T)])
+        raw11 = load_x(1, 1, [(0, T)])
+        for c in range(NCH):
+            gather(0, 1, c)
+            interleave(0, c)
+            if c + 3 < NCH:
+                gather(0, 0, c + 3)
+            if c == 2:
+                cast_x(1, 0, raw10)
+            if c == 3:
+                cast_x(1, 1, raw11)
+        for e in range(6, E + 1):
+            load_w(e)
+        nc.sync.dma_start(out=bias[:], in_=b)
+        for r, pos in enumerate((pos1, pos2, pos3)):
+            nc.sync.dma_start(pos_t[r][:], pos)
+        make_identity(nc, ident[:])
+        for c in range(NCH):
+            gather(1, 0, c)
+            gather(1, 1, c)
+            interleave(1, c)
+
+        def product(wq, e_col, xq, pass_cols, at, n, dst, e):
+            acc = psum.tile([P, 512], F32, name="acc", tag="acc", bufs=4)
+            for g in range(PASSES):
+                wc = slice(e_col + g * N, e_col + (g + 1) * N)
+                xc = slice(g * pass_cols + at, g * pass_cols + at + n)
+                nc.tensor.matmul_mx(acc[:, :n], lhsT=wq[0][:, wc].bitcast(FP8X4), lhsT_scale=wq[1][:, wc],
+                                    rhs=xq[0][:, xc].bitcast(FP8X4), rhs_scale=xq[1][:, xc],
+                                    start=(g == 0), stop=(g == PASSES - 1))
+            nc.scalar.activation(dst, acc[:, :n], ACT.Relu, bias=bias[:, e:e + 1])
+
+        token_chunks = [(0, 512), (512, 1024), (1024, T)]
+        shared_chunks = [(0, CH), (CH, T)]
+        gates = []
+        xs = []
+        for c in range(NCH):
+            wq = quantize(wb[c], EC * 1024, "w", EC * PASSES * N)
+            xq = quantize(xi[c], PASSES * CH * 4, "x", PASSES * CH)
+            for i in range(EC):
+                e = c * EC + i
+                product(wq, i * PASSES * N, xq, CH, i * C, C, y[:, e * C:(e + 1) * C], e)
+            if c < len(token_chunks):
+                a, z = token_chunks[c]
+                gt = ring.tile([P, TOP, z - a], F32, name="gt", tag="wb", bufs=6, align_bytes=AL)
+                nc.sync.dma_start(out=gt[:], in_=gate[:, :, a:z].rearrange("r p t -> p r t"))
+                gates.append(gt)
+            if c < len(shared_chunks):
+                a, z = shared_chunks[c]
+                st = ring.tile([P, PASSES * (z - a) * 4], BF16, name="st", tag="xi", bufs=5, align_bytes=AL)
+                for g in range(PASSES):
+                    dst = st[:, g * (z - a) * 4:(g + 1) * (z - a) * 4].bitcast(F32).rearrange("p (s u) -> p s u", u=2)
+                    src = win[g][:].rearrange("p u t i -> p u (t i)").bitcast(F32)[:, :, a:z].rearrange("p u s -> p s u")
+                    nc.scalar.copy(dst, src)
+                xs.append(st)
+
+        ys = ring.tile([P, T], F32, name="ys", tag="raw", bufs=3, align_bytes=AL)
+        res = ring.tile([P, T], F32, name="res", tag="raw", bufs=3, align_bytes=AL)
+        wq = quantize(wb[NCH], 1024, "w", PASSES * N)
+        for (a, z), st in zip(shared_chunks, xs):
+            xq = quantize(st, PASSES * (z - a) * 4, "x", PASSES * (z - a))
+            at = 0
+            while at < z - a:
+                n = min(512, z - a - at)
+                product(wq, 0, xq, z - a, at, n, ys[:, a + at:a + at + n], E)
+                at += n
+
+        for (a, z), gt in zip(token_chunks, gates):
+            n = z - a
+            pr = ring.tile([P, TOP, n], F32, name="pr", tag="wb", bufs=6, align_bytes=AL)
+            last = z == T
+            for r in range(TOP):
+                nc.vector.tensor_tensor(pr[:, r, :], y[:].indirect(pos_t[r][:, a // 16:z // 16]), gt[:, r, :], ALU.mult)
+                if last and r >= 1:
+                    nc.vector.tensor_tensor(res[:, a:z], ys[:, a:z] if r == 1 else res[:, a:z], pr[:, r - 1, :], ALU.add)
+            if last:
+                nc.vector.tensor_tensor(res[:, a:z], res[:, a:z], pr[:, TOP - 1, :], ALU.add)
+            else:
+                summed = psum.tile([P, 512], F32, name="summed", tag="summed", bufs=2)
+                for h in range(n // P):
+                    blk = slice(h * P, (h + 1) * P)
+                    terms = [ys[:, a + h * P:a + (h + 1) * P]] + [pr[:, r, blk] for r in range(TOP)]
+                    for i, term in enumerate(terms):
+                        nc.tensor.matmul(summed[:, blk], lhsT=term, rhs=ident[:], is_transpose=True,
+                                         start=(i == 0), stop=(i == TOP))
+                turned = ring.tile([P, n], F32, name="turned", tag="gp", bufs=4, align_bytes=AL)
+                nc.scalar.copy(turned[:], summed[:, :n])
+                back = psum.tile([P, 512], F32, name="back", tag="back", bufs=2)
+                for h in range(n // P):
+                    blk = slice(h * P, (h + 1) * P)
+                    nc.tensor.transpose(back[:, blk], turned[:, blk], ident[:])
+                nc.scalar.copy(res[:, a:z], back[:, :n])
+            nc.sync.dma_start(out=out[:, a:z], in_=res[:, a:z])

@@ -23,6 +23,7 @@ EC = 3
 CH = EC * C
 NCH = E // EC
 AL = 64
+G_EXPERTS = 12
 
 
 def widths(total):
@@ -43,13 +44,18 @@ def tile_moe_shr_lin_relu_kernel(tc, xT, w, b, gate, offs, pos1, pos2, pos3, out
         ring = ctx.enter_context(tc.tile_pool(name="ring", bufs=1))
         psum = ctx.enter_context(tc.psum_pool(name="psum", bufs=1))
 
-        def quantize(src, total, tag, width):
-            codes = ring.tile([P, width], U32, name=tag + "_codes", tag=tag + "_codes", bufs=2, align_bytes=AL)
-            scales = ring.tile([P, width], U8, name=tag + "_scales", tag=tag + "_scales", bufs=2, align_bytes=AL)
-            for at, wd in widths(total):
-                cols = slice(at // 4, (at + wd) // 4)
-                nc.vector.quantize_mx(out=codes[:, cols].bitcast(FP8X4), scales=scales[:, cols], in_=src[:, at:at + wd])
-            return codes, scales
+        def quantize(sources):
+            width = sum(n for src, n in sources) // 4
+            codes = ring.tile([P, width], U32, name="codes", tag="codes", bufs=2, align_bytes=AL)
+            scales = ring.tile([P, width], U8, name="scales", tag="scales", bufs=2, align_bytes=AL)
+            base = 0
+            for src, n in sources:
+                for at, wd in widths(n):
+                    cols = slice(base + at // 4, base + (at + wd) // 4)
+                    nc.vector.quantize_mx(out=codes[:, cols].bitcast(FP8X4), scales=scales[:, cols],
+                                          in_=src[:, at:at + wd])
+                base += n // 4
+            return lambda at, n: (codes[:, at:at + n].bitcast(FP8X4), scales[:, at:at + n])
 
         offs_t = keep.tile([P, S // 16], U16, name="offs_t")
         pos_t = [keep.tile([P, T // 16], U16, name="pos%d_t" % r) for r in range(TOP)]
@@ -57,6 +63,8 @@ def tile_moe_shr_lin_relu_kernel(tc, xT, w, b, gate, offs, pos1, pos2, pos3, out
         ident = keep.tile([P, P], F32, name="ident")
         y = keep.tile([P, S], F32, name="y")
         win = [keep.tile([P, 2, T, 2], BF16, name="win%d" % g, align_bytes=AL) for g in range(PASSES)]
+        w_shared = keep.tile([P, 1024], BF16, name="w_shared", align_bytes=AL)
+        xi = [ring.tile([P, 9216], BF16, name="xi", tag="xi", bufs=5, align_bytes=AL) for c in range(NCH)]
         x_rows = xT.rearrange("(g p u i) t -> g u p i t", g=PASSES, p=P, u=2)
 
         def load_x(g, u, pieces):
@@ -68,30 +76,43 @@ def tile_moe_shr_lin_relu_kernel(tc, xT, w, b, gate, offs, pos1, pos2, pos3, out
         def words(g, u):
             return win[g][:, u, :, :].rearrange("p t i -> p (t i)").bitcast(U32)
 
-        wb = {}
-
         def load_w(e):
             raw = ring.tile([P, PASSES, 4, N], F32, name="wraw", tag="wraw", bufs=4)
             nc.sync.dma_start(out=raw[:], in_=w[e].rearrange("(g p j) n -> p g j n", g=PASSES, p=P))
             c, i = divmod(e, EC)
-            if i == 0:
-                wb[c] = ring.tile([P, EC * PASSES * N * 4], BF16, name="wb", tag="wb", bufs=6, align_bytes=AL)
-            dst = wb[c][:, i * 1024:(i + 1) * 1024].rearrange("p (g n j) -> p g n j", g=PASSES, j=4)
-            nc.gpsimd.tensor_scalar(dst, raw[:].rearrange("p g j n -> p g n j"), 1.0, 0.0, ALU.mult, ALU.add)
+            dst = xi[c][:, (i + 1) * 1024:(i + 2) * 1024] if e < E else w_shared[:]
+            if e < G_EXPERTS:
+                nc.gpsimd.tensor_scalar(dst.rearrange("p (g n j) -> p g n j", g=PASSES, j=4),
+                                        raw[:].rearrange("p g j n -> p g n j"), 1.0, 0.0, ALU.mult, ALU.add)
+            else:
+                nc.scalar.copy(dst.rearrange("p (g c i j) -> p g c j i", g=PASSES, i=4, j=4),
+                               raw[:].rearrange("p g j (c i) -> p g c j i", i=4))
 
         gp = {}
-        xi = {}
 
         def gather(g, u, c):
             if u == 0:
-                gp[g, c] = ring.tile([P, 2, CH], U32, name="gp", tag="gp", bufs=4, align_bytes=AL)
+                gp[g, c] = ring.tile([P, 2, CH], U32, name="gp", tag="gp", bufs=5, align_bytes=AL)
             nc.vector.tensor_copy(gp[g, c][:, u, :], words(g, u).indirect(offs_t[:, c * CH // 16:(c + 1) * CH // 16]))
 
         def interleave(g, c):
+            src = gp[g, c][:].bitcast(F32)
             if g == 0:
-                xi[c] = ring.tile([P, PASSES * CH * 4], BF16, name="xi", tag="xi", bufs=5, align_bytes=AL)
-            dst = xi[c][:, g * CH * 4:(g + 1) * CH * 4].bitcast(F32).rearrange("p (s u) -> p s u", u=2)
-            nc.scalar.copy(dst, gp[g, c][:].bitcast(F32).rearrange("p u s -> p s u"))
+                dst = xi[c][:, 5120:8192].bitcast(F32).rearrange("p (s u) -> p s u", u=2)
+                nc.scalar.copy(dst, src.rearrange("p u s -> p s u"))
+            else:
+                two = xi[c][:, 0:8192].bitcast(F32).rearrange("p (i s u) -> p i s u", i=2, u=2)[:, :, 0:C, :]
+                nc.scalar.copy(two, src[:, :, 0:2 * C].rearrange("p u (i s) -> p i s u", i=2))
+                nc.scalar.copy(xi[c][:, 8192:].bitcast(F32).rearrange("p (s u) -> p s u", u=2),
+                               src[:, :, 2 * C:].rearrange("p u s -> p s u"))
+
+        xs = []
+
+        def relay(g):
+            st = ring.tile([P, T * 4], BF16, name="st", tag="raw", bufs=3, align_bytes=AL)
+            nc.scalar.copy(st[:].bitcast(F32).rearrange("p (s u) -> p s u", u=2),
+                           win[g][:].rearrange("p u t i -> p u (t i)").bitcast(F32).rearrange("p u s -> p s u"))
+            xs.append(st)
 
         def cast_x(g, u, raw):
             nc.scalar.activation(win[g][:, u, :, :], raw[:].rearrange("p i t -> p t i"), ACT.Copy)
@@ -103,22 +124,22 @@ def tile_moe_shr_lin_relu_kernel(tc, xT, w, b, gate, offs, pos1, pos2, pos3, out
         for a, z in first:
             nc.vector.tensor_copy(win[0][:, 0, a:z, :], raw00[:, :, a:z].rearrange("p i t -> p t i"))
         cast_x(0, 1, raw01)
-        for e in range(6):
-            load_w(e)
+        load_w(0)
+        raw10 = load_x(1, 0, [(0, T)])
+        load_w(1)
+        raw11 = load_x(1, 1, [(0, T)])
+        relay(0)
+        cast_x(1, 0, raw10)
         for c in range(3):
             gather(0, 0, c)
-        raw10 = load_x(1, 0, [(0, T)])
-        raw11 = load_x(1, 1, [(0, T)])
         for c in range(NCH):
             gather(0, 1, c)
             interleave(0, c)
             if c + 3 < NCH:
                 gather(0, 0, c + 3)
-            if c == 2:
-                cast_x(1, 0, raw10)
-            if c == 3:
+            if c == 0:
                 cast_x(1, 1, raw11)
-        for e in range(6, E + 1):
+        for e in range(2, G_EXPERTS):
             load_w(e)
         nc.sync.dma_start(out=bias[:], in_=b)
         for r, pos in enumerate((pos1, pos2, pos3)):
@@ -128,73 +149,59 @@ def tile_moe_shr_lin_relu_kernel(tc, xT, w, b, gate, offs, pos1, pos2, pos3, out
             gather(1, 0, c)
             gather(1, 1, c)
             interleave(1, c)
+            if c == 0:
+                relay(1)
+            if c in (2, 3):
+                for e in range(G_EXPERTS + 2 * (c - 2), min(E + 1, G_EXPERTS + 2 * (c - 1))):
+                    load_w(e)
 
-        def product(wq, e_col, xq, pass_cols, at, n, dst, e):
-            acc = psum.tile([P, 512], F32, name="acc", tag="acc", bufs=4)
+        def product(ws, xq, n, dst, e):
+            acc = psum.tile([P, 512], F32, name="acc", tag="bank", bufs=8)
             for g in range(PASSES):
-                wc = slice(e_col + g * N, e_col + (g + 1) * N)
-                xc = slice(g * pass_cols + at, g * pass_cols + at + n)
-                nc.tensor.matmul_mx(acc[:, :n], lhsT=wq[0][:, wc].bitcast(FP8X4), lhsT_scale=wq[1][:, wc],
-                                    rhs=xq[0][:, xc].bitcast(FP8X4), rhs_scale=xq[1][:, xc],
+                nc.tensor.matmul_mx(acc[:, :n], lhsT=ws[g][0], lhsT_scale=ws[g][1], rhs=xq[g][0], rhs_scale=xq[g][1],
                                     start=(g == 0), stop=(g == PASSES - 1))
             nc.scalar.activation(dst, acc[:, :n], ACT.Relu, bias=bias[:, e:e + 1])
 
-        token_chunks = [(0, 512), (512, 1024), (1024, T)]
-        shared_chunks = [(0, CH), (CH, T)]
-        gates = []
-        xs = []
+        token_chunks = [(0, 384), (384, 640), (640, 896), (896, 1152), (1152, T)]
         for c in range(NCH):
-            wq = quantize(wb[c], EC * 1024, "w", EC * PASSES * N)
-            xq = quantize(xi[c], PASSES * CH * 4, "x", PASSES * CH)
+            q = quantize([(xi[c], 9216)])
             for i in range(EC):
                 e = c * EC + i
-                product(wq, i * PASSES * N, xq, CH, i * C, C, y[:, e * C:(e + 1) * C], e)
-            if c < len(token_chunks):
-                a, z = token_chunks[c]
-                gt = ring.tile([P, TOP, z - a], F32, name="gt", tag="wb", bufs=6, align_bytes=AL)
-                nc.sync.dma_start(out=gt[:], in_=gate[:, :, a:z].rearrange("r p t -> p r t"))
-                gates.append(gt)
-            if c < len(shared_chunks):
-                a, z = shared_chunks[c]
-                st = ring.tile([P, PASSES * (z - a) * 4], BF16, name="st", tag="xi", bufs=5, align_bytes=AL)
-                for g in range(PASSES):
-                    dst = st[:, g * (z - a) * 4:(g + 1) * (z - a) * 4].bitcast(F32).rearrange("p (s u) -> p s u", u=2)
-                    src = win[g][:].rearrange("p u t i -> p u (t i)").bitcast(F32)[:, :, a:z].rearrange("p u s -> p s u")
-                    nc.scalar.copy(dst, src)
-                xs.append(st)
+                ws = [q((i + 1) * 256 + g * N, N) for g in range(PASSES)]
+                product(ws, [q(1280 + i * C, C), q(i * 1024, C)], C, y[:, e * C:(e + 1) * C], e)
+        gates = ring.tile([P, TOP, T], F32, name="gates", tag="xi", bufs=5, align_bytes=AL)
+        nc.sync.dma_start(out=gates[:], in_=gate.rearrange("r p t -> p r t"))
 
         ys = ring.tile([P, T], F32, name="ys", tag="raw", bufs=3, align_bytes=AL)
         res = ring.tile([P, T], F32, name="res", tag="raw", bufs=3, align_bytes=AL)
-        wq = quantize(wb[NCH], 1024, "w", PASSES * N)
-        for (a, z), st in zip(shared_chunks, xs):
-            xq = quantize(st, PASSES * (z - a) * 4, "x", PASSES * (z - a))
-            at = 0
-            while at < z - a:
-                n = min(512, z - a - at)
-                product(wq, 0, xq, z - a, at, n, ys[:, a + at:a + at + n], E)
-                at += n
+        q0 = quantize([(xs[0], T * 4), (w_shared, 1024)])
+        q1 = quantize([(xs[1], T * 4)])
+        for at in range(0, T, 512):
+            n = min(512, T - at)
+            product([q0(T + g * N, N) for g in range(PASSES)], [q0(at, n), q1(at, n)], n, ys[:, at:at + n], E)
 
-        for (a, z), gt in zip(token_chunks, gates):
+        for a, z in token_chunks:
             n = z - a
-            pr = ring.tile([P, TOP, n], F32, name="pr", tag="wb", bufs=6, align_bytes=AL)
+            pr = ring.tile([P, TOP, n], F32, name="pr", tag="xi", bufs=5, align_bytes=AL)
             last = z == T
             for r in range(TOP):
-                nc.vector.tensor_tensor(pr[:, r, :], y[:].indirect(pos_t[r][:, a // 16:z // 16]), gt[:, r, :], ALU.mult)
+                nc.vector.tensor_tensor(pr[:, r, :], y[:].indirect(pos_t[r][:, a // 16:z // 16]), gates[:, r, a:z],
+                                        ALU.mult)
                 if last and r >= 1:
                     nc.vector.tensor_tensor(res[:, a:z], ys[:, a:z] if r == 1 else res[:, a:z], pr[:, r - 1, :], ALU.add)
             if last:
                 nc.vector.tensor_tensor(res[:, a:z], res[:, a:z], pr[:, TOP - 1, :], ALU.add)
             else:
-                summed = psum.tile([P, 512], F32, name="summed", tag="summed", bufs=2)
+                summed = psum.tile([P, 512], F32, name="summed", tag="bank", bufs=8)
                 for h in range(n // P):
                     blk = slice(h * P, (h + 1) * P)
                     terms = [ys[:, a + h * P:a + (h + 1) * P]] + [pr[:, r, blk] for r in range(TOP)]
                     for i, term in enumerate(terms):
                         nc.tensor.matmul(summed[:, blk], lhsT=term, rhs=ident[:], is_transpose=True,
                                          start=(i == 0), stop=(i == TOP))
-                turned = ring.tile([P, n], F32, name="turned", tag="gp", bufs=4, align_bytes=AL)
+                turned = ring.tile([P, n], F32, name="turned", tag="gp", bufs=5, align_bytes=AL)
                 nc.scalar.copy(turned[:], summed[:, :n])
-                back = psum.tile([P, 512], F32, name="back", tag="back", bufs=2)
+                back = psum.tile([P, 512], F32, name="back", tag="bank", bufs=8)
                 for h in range(n // P):
                     blk = slice(h * P, (h + 1) * P)
                     nc.tensor.transpose(back[:, blk], turned[:, blk], ident[:])

@@ -23,7 +23,8 @@ EC = 3
 CH = EC * C
 NCH = E // EC
 AL = 64
-G_EXPERTS = 12
+V_EXPERTS = 7
+G_EXPERTS = 16
 
 
 def widths(total):
@@ -63,6 +64,7 @@ def tile_moe_shr_lin_relu_kernel(tc, xT, w, b, gate, offs, pos1, pos2, pos3, out
         ident = keep.tile([P, P], F32, name="ident")
         y = keep.tile([P, S], F32, name="y")
         win = [keep.tile([P, 2, T, 2], BF16, name="win%d" % g, align_bytes=AL) for g in range(PASSES)]
+        rows = keep.tile([P, 2, T], BF16, name="rows", align_bytes=AL)
         w_shared = keep.tile([P, 1024], BF16, name="w_shared", align_bytes=AL)
         xi = [ring.tile([P, 9216], BF16, name="xi", tag="xi", bufs=5, align_bytes=AL) for c in range(NCH)]
         x_rows = xT.rearrange("(g p u i) t -> g u p i t", g=PASSES, p=P, u=2)
@@ -90,10 +92,21 @@ def tile_moe_shr_lin_relu_kernel(tc, xT, w, b, gate, offs, pos1, pos2, pos3, out
 
         gp = {}
 
-        def gather(g, u, c):
-            if u == 0:
-                gp[g, c] = ring.tile([P, 2, CH], U32, name="gp", tag="gp", bufs=5, align_bytes=AL)
-            nc.vector.tensor_copy(gp[g, c][:, u, :], words(g, u).indirect(offs_t[:, c * CH // 16:(c + 1) * CH // 16]))
+        def planes(g, c):
+            if (g, c) not in gp:
+                gp[g, c] = ring.tile([P, 2, CH], U32, name="gp", tag="gp", bufs=6, align_bytes=AL)
+            return gp[g, c]
+
+        def gather(g, u, c, n=CH):
+            nc.vector.tensor_copy(planes(g, c)[:, u, :n],
+                                  words(g, u).indirect(offs_t[:, c * CH // 16:(c * CH + n) // 16]))
+
+        def gather_rows(e):
+            c, i = divmod(e, EC)
+            dst = planes(0, c)[:, 0, i * C:(i + 1) * C].bitcast(BF16).rearrange("p (s i) -> p s i", i=2)
+            for i in range(2):
+                nc.scalar.activation(dst[:, :, i], rows[:, i, :].indirect(offs_t[:, e * C // 16:(e + 1) * C // 16]),
+                                     ACT.Copy)
 
         def interleave(g, c):
             src = gp[g, c][:].bitcast(F32)
@@ -114,31 +127,41 @@ def tile_moe_shr_lin_relu_kernel(tc, xT, w, b, gate, offs, pos1, pos2, pos3, out
                            win[g][:].rearrange("p u t i -> p u (t i)").bitcast(F32).rearrange("p u s -> p s u"))
             xs.append(st)
 
-        def cast_x(g, u, raw):
-            nc.scalar.activation(win[g][:, u, :, :], raw[:].rearrange("p i t -> p t i"), ACT.Copy)
+        def cast_x(g, u, raw, a=0, z=T):
+            nc.scalar.activation(win[g][:, u, a:z, :], raw[:, :, a:z].rearrange("p i t -> p t i"), ACT.Copy)
 
         first = [(0, 512), (512, 1024), (1024, T)]
         raw00 = load_x(0, 0, first)
         nc.sync.dma_start(offs_t[:], offs)
-        raw01 = load_x(0, 1, [(0, T)])
+        raw01 = load_x(0, 1, first)
         for a, z in first:
             nc.vector.tensor_copy(win[0][:, 0, a:z, :], raw00[:, :, a:z].rearrange("p i t -> p t i"))
-        cast_x(0, 1, raw01)
+            nc.scalar.activation(rows[:, :, a:z], raw00[:, :, a:z], ACT.Copy)
+        for a, z in first:
+            cast_x(0, 1, raw01, a, z)
         load_w(0)
         raw10 = load_x(1, 0, [(0, T)])
         load_w(1)
         raw11 = load_x(1, 1, [(0, T)])
-        relay(0)
-        cast_x(1, 0, raw10)
-        for c in range(3):
-            gather(0, 0, c)
+        for c in range(NCH):
+            n = min(CH, V_EXPERTS * C - c * CH)
+            if n > 0:
+                gather(0, 0, c, n)
         for c in range(NCH):
             gather(0, 1, c)
+        by_scalar = list(range(V_EXPERTS, E))
+        for e in by_scalar[:3]:
+            gather_rows(e)
+        cast_x(1, 0, raw10)
+        interleave(0, 0)
+        cast_x(1, 1, raw11)
+        interleave(0, 1)
+        interleave(0, 2)
+        for c in range(3, NCH):
+            for e in by_scalar[3:]:
+                if e // EC == c:
+                    gather_rows(e)
             interleave(0, c)
-            if c + 3 < NCH:
-                gather(0, 0, c + 3)
-            if c == 0:
-                cast_x(1, 1, raw11)
         for e in range(2, G_EXPERTS):
             load_w(e)
         nc.sync.dma_start(out=bias[:], in_=b)
@@ -149,11 +172,6 @@ def tile_moe_shr_lin_relu_kernel(tc, xT, w, b, gate, offs, pos1, pos2, pos3, out
             gather(1, 0, c)
             gather(1, 1, c)
             interleave(1, c)
-            if c == 0:
-                relay(1)
-            if c in (2, 3):
-                for e in range(G_EXPERTS + 2 * (c - 2), min(E + 1, G_EXPERTS + 2 * (c - 1))):
-                    load_w(e)
 
         def product(ws, xq, n, dst, e):
             acc = psum.tile([P, 512], F32, name="acc", tag="bank", bufs=8)
@@ -169,8 +187,11 @@ def tile_moe_shr_lin_relu_kernel(tc, xT, w, b, gate, offs, pos1, pos2, pos3, out
                 e = c * EC + i
                 ws = [q((i + 1) * 256 + g * N, N) for g in range(PASSES)]
                 product(ws, [q(1280 + i * C, C), q(i * 1024, C)], C, y[:, e * C:(e + 1) * C], e)
-        gates = ring.tile([P, TOP, T], F32, name="gates", tag="xi", bufs=5, align_bytes=AL)
-        nc.sync.dma_start(out=gates[:], in_=gate.rearrange("r p t -> p r t"))
+            if c == 0:
+                gates = ring.tile([P, TOP, T], F32, name="gates", tag="xi", bufs=5, align_bytes=AL)
+                nc.scalar.dma_start(out=gates[:], in_=gate.rearrange("r p t -> p r t"))
+            if c < PASSES:
+                relay(c)
 
         ys = ring.tile([P, T], F32, name="ys", tag="raw", bufs=3, align_bytes=AL)
         res = ring.tile([P, T], F32, name="res", tag="raw", bufs=3, align_bytes=AL)
@@ -199,7 +220,7 @@ def tile_moe_shr_lin_relu_kernel(tc, xT, w, b, gate, offs, pos1, pos2, pos3, out
                     for i, term in enumerate(terms):
                         nc.tensor.matmul(summed[:, blk], lhsT=term, rhs=ident[:], is_transpose=True,
                                          start=(i == 0), stop=(i == TOP))
-                turned = ring.tile([P, n], F32, name="turned", tag="gp", bufs=5, align_bytes=AL)
+                turned = ring.tile([P, n], F32, name="turned", tag="gp", bufs=6, align_bytes=AL)
                 nc.scalar.copy(turned[:], summed[:, :n])
                 back = psum.tile([P, 512], F32, name="back", tag="bank", bufs=8)
                 for h in range(n // P):

@@ -23,8 +23,8 @@ EC = 3
 CH = EC * C
 NCH = E // EC
 AL = 64
-V_EXPERTS = 7
-G_EXPERTS = 16
+V_EXPERTS = 9
+G_EXPERTS = 14
 
 
 def widths(total):
@@ -69,10 +69,10 @@ def tile_moe_shr_lin_relu_kernel(tc, xT, w, b, gate, offs, pos1, pos2, pos3, out
         xi = [ring.tile([P, 9216], BF16, name="xi", tag="xi", bufs=5, align_bytes=AL) for c in range(NCH)]
         x_rows = xT.rearrange("(g p u i) t -> g u p i t", g=PASSES, p=P, u=2)
 
-        def load_x(g, u, pieces):
+        def load_x(g, u, pieces, queue):
             raw = ring.tile([P, 2, T], F32, name="raw", tag="raw", bufs=3, align_bytes=AL)
             for a, z in pieces:
-                nc.sync.dma_start(out=raw[:, :, a:z], in_=x_rows[g, u][:, :, a:z])
+                queue.dma_start(out=raw[:, :, a:z], in_=x_rows[g, u][:, :, a:z])
             return raw
 
         def words(g, u):
@@ -131,18 +131,17 @@ def tile_moe_shr_lin_relu_kernel(tc, xT, w, b, gate, offs, pos1, pos2, pos3, out
             nc.scalar.activation(win[g][:, u, a:z, :], raw[:, :, a:z].rearrange("p i t -> p t i"), ACT.Copy)
 
         first = [(0, 512), (512, 1024), (1024, T)]
-        raw00 = load_x(0, 0, first)
+        raw00 = load_x(0, 0, first, nc.sync)
         nc.sync.dma_start(offs_t[:], offs)
-        raw01 = load_x(0, 1, first)
+        raw01 = load_x(0, 1, first, nc.sync)
         for a, z in first:
             nc.vector.tensor_copy(win[0][:, 0, a:z, :], raw00[:, :, a:z].rearrange("p i t -> p t i"))
             nc.scalar.activation(rows[:, :, a:z], raw00[:, :, a:z], ACT.Copy)
         for a, z in first:
             cast_x(0, 1, raw01, a, z)
-        load_w(0)
-        raw10 = load_x(1, 0, [(0, T)])
-        load_w(1)
-        raw11 = load_x(1, 1, [(0, T)])
+        for e in range(3):
+            load_w(e)
+        raw10 = load_x(1, 0, [(0, T)], nc.sync)
         for c in range(NCH):
             n = min(CH, V_EXPERTS * C - c * CH)
             if n > 0:
@@ -152,17 +151,16 @@ def tile_moe_shr_lin_relu_kernel(tc, xT, w, b, gate, offs, pos1, pos2, pos3, out
         by_scalar = list(range(V_EXPERTS, E))
         for e in by_scalar[:3]:
             gather_rows(e)
+        raw11 = load_x(1, 1, [(0, T)], nc.scalar)
         cast_x(1, 0, raw10)
-        interleave(0, 0)
-        cast_x(1, 1, raw11)
-        interleave(0, 1)
-        interleave(0, 2)
-        for c in range(3, NCH):
+        for c in range(NCH):
             for e in by_scalar[3:]:
                 if e // EC == c:
                     gather_rows(e)
             interleave(0, c)
-        for e in range(2, G_EXPERTS):
+            if c == 3:
+                cast_x(1, 1, raw11)
+        for e in range(3, G_EXPERTS):
             load_w(e)
         nc.sync.dma_start(out=bias[:], in_=b)
         for r, pos in enumerate((pos1, pos2, pos3)):
@@ -170,6 +168,7 @@ def tile_moe_shr_lin_relu_kernel(tc, xT, w, b, gate, offs, pos1, pos2, pos3, out
         make_identity(nc, ident[:])
         for c in range(NCH):
             gather(1, 0, c)
+        for c in range(NCH):
             gather(1, 1, c)
             interleave(1, c)
 
@@ -192,6 +191,7 @@ def tile_moe_shr_lin_relu_kernel(tc, xT, w, b, gate, offs, pos1, pos2, pos3, out
                 nc.scalar.dma_start(out=gates[:], in_=gate.rearrange("r p t -> p r t"))
             if c < PASSES:
                 relay(c)
+                load_w(G_EXPERTS + c)
 
         ys = ring.tile([P, T], F32, name="ys", tag="raw", bufs=3, align_bytes=AL)
         res = ring.tile([P, T], F32, name="res", tag="raw", bufs=3, align_bytes=AL)

@@ -23,7 +23,7 @@ EC = 3
 CH = EC * C
 NCH = E // EC
 AL = 64
-V_EXPERTS = 9
+V_EXPERTS = 8
 G_EXPERTS = 14
 
 
@@ -179,7 +179,7 @@ def tile_moe_shr_lin_relu_kernel(tc, xT, w, b, gate, offs, pos1, pos2, pos3, out
                                     start=(g == 0), stop=(g == PASSES - 1))
             nc.scalar.activation(dst, acc[:, :n], ACT.Relu, bias=bias[:, e:e + 1])
 
-        token_chunks = [(0, 384), (384, 640), (640, 896), (896, 1152), (1152, T)]
+        token_chunks = [(0, 384), (384, 768), (768, 1024), (1024, T)]
         for c in range(NCH):
             q = quantize([(xi[c], 9216)])
             for i in range(EC):

from contextlib import ExitStack

import concourse.mybir as mybir
from concourse.masks import make_identity

K, T, E, C, N = 1024, 1280, 15, 256, 128
TOP = 3
S = E * C
FLOPS = 2 * K * N * (S + T)

F32 = mybir.dt.float32
BF16 = mybir.dt.bfloat16
U32 = mybir.dt.uint32
U16 = mybir.dt.uint16
U8 = mybir.dt.uint8
FP8X4 = mybir.dt.float8_e4m3fn_x4
ACT = mybir.ActivationFunctionType
ALU = mybir.AluOpType

P = 128
PASSES = 2
EC = 3
CH = EC * C
NCH = E // EC
AL = 64
V_EXPERTS = 8
G_EXPERTS = 14


def widths(total):
    out, at = [], 0
    while at < total:
        w = 4096
        while w > total - at:
            w //= 2
        out.append((at, w))
        at += w
    return out


def tile_moe_shr_lin_relu_kernel(tc, xT, w, b, gate, offs, pos1, pos2, pos3, out):
    nc = tc.nc
    with ExitStack() as ctx:
        keep = ctx.enter_context(tc.tile_pool(name="keep", bufs=1))
        ring = ctx.enter_context(tc.tile_pool(name="ring", bufs=1))
        psum = ctx.enter_context(tc.psum_pool(name="psum", bufs=1))

        def quantize(sources):
            width = sum(n for src, n in sources) // 4
            codes = ring.tile([P, width], U32, name="codes", tag="codes", bufs=2, align_bytes=AL)
            scales = ring.tile([P, width], U8, name="scales", tag="scales", bufs=2, align_bytes=AL)
            base = 0
            for src, n in sources:
                for at, wd in widths(n):
                    cols = slice(base + at // 4, base + (at + wd) // 4)
                    nc.vector.quantize_mx(out=codes[:, cols].bitcast(FP8X4), scales=scales[:, cols],
                                          in_=src[:, at:at + wd])
                base += n // 4
            return lambda at, n: (codes[:, at:at + n].bitcast(FP8X4), scales[:, at:at + n])

        offs_t = keep.tile([P, S // 16], U16, name="offs_t")
        pos_t = [keep.tile([P, T // 16], U16, name="pos%d_t" % r) for r in range(TOP)]
        bias = keep.tile([P, E + 1], F32, name="bias")
        ident = keep.tile([P, P], F32, name="ident")
        y = keep.tile([P, S], F32, name="y")
        win = [keep.tile([P, 2, T, 2], BF16, name="win%d" % g, align_bytes=AL) for g in range(PASSES)]
        rows = keep.tile([P, 2, T], BF16, name="rows", align_bytes=AL)
        w_shared = keep.tile([P, 1024], BF16, name="w_shared", align_bytes=AL)
        xi = [ring.tile([P, 9216], BF16, name="xi", tag="xi", bufs=5, align_bytes=AL) for c in range(NCH)]
        x_rows = xT.rearrange("(g p u i) t -> g u p i t", g=PASSES, p=P, u=2)

        def load_x(g, u, pieces, queue):
            raw = ring.tile([P, 2, T], F32, name="raw", tag="raw", bufs=3, align_bytes=AL)
            for a, z in pieces:
                queue.dma_start(out=raw[:, :, a:z], in_=x_rows[g, u][:, :, a:z])
            return raw

        def words(g, u):
            return win[g][:, u, :, :].rearrange("p t i -> p (t i)").bitcast(U32)

        def load_w(e):
            raw = ring.tile([P, PASSES, 4, N], F32, name="wraw", tag="wraw", bufs=4)
            nc.sync.dma_start(out=raw[:], in_=w[e].rearrange("(g p j) n -> p g j n", g=PASSES, p=P))
            c, i = divmod(e, EC)
            dst = xi[c][:, (i + 1) * 1024:(i + 2) * 1024] if e < E else w_shared[:]
            if e < G_EXPERTS:
                nc.gpsimd.tensor_scalar(dst.rearrange("p (g n j) -> p g n j", g=PASSES, j=4),
                                        raw[:].rearrange("p g j n -> p g n j"), 1.0, 0.0, ALU.mult, ALU.add)
            else:
                nc.scalar.copy(dst.rearrange("p (g c i j) -> p g c j i", g=PASSES, i=4, j=4),
                               raw[:].rearrange("p g j (c i) -> p g c j i", i=4))

        gp = {}

        def planes(g, c):
            if (g, c) not in gp:
                gp[g, c] = ring.tile([P, 2, CH], U32, name="gp", tag="gp", bufs=6, align_bytes=AL)
            return gp[g, c]

        def gather(g, u, c, n=CH):
            nc.vector.tensor_copy(planes(g, c)[:, u, :n],
                                  words(g, u).indirect(offs_t[:, c * CH // 16:(c * CH + n) // 16]))

        def gather_rows(e):
            c, i = divmod(e, EC)
            dst = planes(0, c)[:, 0, i * C:(i + 1) * C].bitcast(BF16).rearrange("p (s i) -> p s i", i=2)
            for i in range(2):
                nc.scalar.activation(dst[:, :, i], rows[:, i, :].indirect(offs_t[:, e * C // 16:(e + 1) * C // 16]),
                                     ACT.Copy)

        def interleave(g, c):
            src = gp[g, c][:].bitcast(F32)
            if g == 0:
                dst = xi[c][:, 5120:8192].bitcast(F32).rearrange("p (s u) -> p s u", u=2)
                nc.scalar.copy(dst, src.rearrange("p u s -> p s u"))
            else:
                two = xi[c][:, 0:8192].bitcast(F32).rearrange("p (i s u) -> p i s u", i=2, u=2)[:, :, 0:C, :]
                nc.scalar.copy(two, src[:, :, 0:2 * C].rearrange("p u (i s) -> p i s u", i=2))
                nc.scalar.copy(xi[c][:, 8192:].bitcast(F32).rearrange("p (s u) -> p s u", u=2),
                               src[:, :, 2 * C:].rearrange("p u s -> p s u"))

        xs = []

        def relay(g):
            st = ring.tile([P, T * 4], BF16, name="st", tag="raw", bufs=3, align_bytes=AL)
            nc.scalar.copy(st[:].bitcast(F32).rearrange("p (s u) -> p s u", u=2),
                           win[g][:].rearrange("p u t i -> p u (t i)").bitcast(F32).rearrange("p u s -> p s u"))
            xs.append(st)

        def cast_x(g, u, raw, a=0, z=T):
            nc.scalar.activation(win[g][:, u, a:z, :], raw[:, :, a:z].rearrange("p i t -> p t i"), ACT.Copy)

        first = [(0, 512), (512, 1024), (1024, T)]
        raw00 = load_x(0, 0, first, nc.sync)
        nc.sync.dma_start(offs_t[:], offs)
        raw01 = load_x(0, 1, first, nc.sync)
        for a, z in first:
            nc.vector.tensor_copy(win[0][:, 0, a:z, :], raw00[:, :, a:z].rearrange("p i t -> p t i"))
            nc.scalar.activation(rows[:, :, a:z], raw00[:, :, a:z], ACT.Copy)
        for a, z in first:
            cast_x(0, 1, raw01, a, z)
        for e in range(3):
            load_w(e)
        raw10 = load_x(1, 0, [(0, T)], nc.sync)
        for c in range(NCH):
            n = min(CH, V_EXPERTS * C - c * CH)
            if n > 0:
                gather(0, 0, c, n)
        for c in range(NCH):
            gather(0, 1, c)
        by_scalar = list(range(V_EXPERTS, E))
        for e in by_scalar[:3]:
            gather_rows(e)
        raw11 = load_x(1, 1, [(0, T)], nc.scalar)
        cast_x(1, 0, raw10)
        for c in range(NCH):
            for e in by_scalar[3:]:
                if e // EC == c:
                    gather_rows(e)
            interleave(0, c)
            if c == 3:
                cast_x(1, 1, raw11)
        for e in range(3, G_EXPERTS):
            load_w(e)
        nc.sync.dma_start(out=bias[:], in_=b)
        for r, pos in enumerate((pos1, pos2, pos3)):
            nc.sync.dma_start(pos_t[r][:], pos)
        make_identity(nc, ident[:])
        for c in range(NCH):
            gather(1, 0, c)
        for c in range(NCH):
            gather(1, 1, c)
            interleave(1, c)

        def product(ws, xq, n, dst, e):
            acc = psum.tile([P, 512], F32, name="acc", tag="bank", bufs=8)
            for g in range(PASSES):
                nc.tensor.matmul_mx(acc[:, :n], lhsT=ws[g][0], lhsT_scale=ws[g][1], rhs=xq[g][0], rhs_scale=xq[g][1],
                                    start=(g == 0), stop=(g == PASSES - 1))
            nc.scalar.activation(dst, acc[:, :n], ACT.Relu, bias=bias[:, e:e + 1])

        token_chunks = [(0, 384), (384, 768), (768, 1024), (1024, T)]
        for c in range(NCH):
            q = quantize([(xi[c], 9216)])
            for i in range(EC):
                e = c * EC + i
                ws = [q((i + 1) * 256 + g * N, N) for g in range(PASSES)]
                product(ws, [q(1280 + i * C, C), q(i * 1024, C)], C, y[:, e * C:(e + 1) * C], e)
            if c == 0:
                gates = ring.tile([P, TOP, T], F32, name="gates", tag="xi", bufs=5, align_bytes=AL)
                nc.scalar.dma_start(out=gates[:], in_=gate.rearrange("r p t -> p r t"))
            if c < PASSES:
                relay(c)
                load_w(G_EXPERTS + c)

        ys = ring.tile([P, T], F32, name="ys", tag="raw", bufs=3, align_bytes=AL)
        res = ring.tile([P, T], F32, name="res", tag="raw", bufs=3, align_bytes=AL)
        q0 = quantize([(xs[0], T * 4), (w_shared, 1024)])
        q1 = quantize([(xs[1], T * 4)])
        for at in range(0, T, 512):
            n = min(512, T - at)
            product([q0(T + g * N, N) for g in range(PASSES)], [q0(at, n), q1(at, n)], n, ys[:, at:at + n], E)

        for a, z in token_chunks:
            n = z - a
            pr = ring.tile([P, TOP, n], F32, name="pr", tag="xi", bufs=5, align_bytes=AL)
            last = z == T
            for r in range(TOP):
                nc.vector.tensor_tensor(pr[:, r, :], y[:].indirect(pos_t[r][:, a // 16:z // 16]), gates[:, r, a:z],
                                        ALU.mult)
                if last and r >= 1:
                    nc.vector.tensor_tensor(res[:, a:z], ys[:, a:z] if r == 1 else res[:, a:z], pr[:, r - 1, :], ALU.add)
            if last:
                nc.vector.tensor_tensor(res[:, a:z], res[:, a:z], pr[:, TOP - 1, :], ALU.add)
            else:
                summed = psum.tile([P, 512], F32, name="summed", tag="bank", bufs=8)
                for h in range(n // P):
                    blk = slice(h * P, (h + 1) * P)
                    terms = [ys[:, a + h * P:a + (h + 1) * P]] + [pr[:, r, blk] for r in range(TOP)]
                    for i, term in enumerate(terms):
                        nc.tensor.matmul(summed[:, blk], lhsT=term, rhs=ident[:], is_transpose=True,
                                         start=(i == 0), stop=(i == TOP))
                turned = ring.tile([P, n], F32, name="turned", tag="gp", bufs=6, align_bytes=AL)
                nc.scalar.copy(turned[:], summed[:, :n])
                back = psum.tile([P, 512], F32, name="back", tag="bank", bufs=8)
                for h in range(n // P):
                    blk = slice(h * P, (h + 1) * P)
                    nc.tensor.transpose(back[:, blk], turned[:, blk], ident[:])
                nc.scalar.copy(res[:, a:z], back[:, :n])
            nc.sync.dma_start(out=out[:, a:z], in_=res[:, a:z])
